import numpy as np, ml_dtypes
CORES = [24,26,29,31,48,50,53,55]
N = 8
import mx_ref
NC = 128
BF = ml_dtypes.bfloat16
def setup_inputs(rng):
    def f(*shape):
        return mx_ref.flush((rng.standard_normal(shape, dtype=np.float32) * np.exp2(rng.integers(-2, 3, shape[:-1] + (1,)))).astype(BF))
    return {"x": f(N, 128, 512), "rt": f(N, 128, 512), "w": f(N, 128, 4 * NC)}
def setup_inputs_blocks(rng):
    d = setup_inputs(rng)
    for k in ("x", "rt", "w"): d[k] = mx_ref.spread(d[k], rng, 4)
    return d
def setup_inputs_wide(rng):
    d = setup_inputs(rng)
    for k in ("x", "rt", "w"): d[k] = mx_ref.flush((d[k].astype(np.float32) * np.exp2(rng.integers(-6, 7, (N, 1, 1))).astype(np.float32)).astype(BF))
    return d
def setup_inputs_near(rng):
    d = setup_inputs(rng); v = d["rt"].astype(np.float32).reshape(N, 128, -1, 4)
    d["rt"] = mx_ref.flush((v[:, :, :1] + v / 64).reshape(d["rt"].shape).astype(BF))
    return d
def setup_inputs_twins(rng):
    d = setup_inputs(rng); v = d["rt"].reshape(N, 128, -1, 4).copy()
    v[:, :, 1] = v[:, :, 0]
    d["rt"] = v.reshape(d["rt"].shape)
    return d
def reference(x, rt, w):
    W = [mx_ref.quantize(w[e]) for e in range(N)]
    y = np.zeros((N, 128, NC), np.float32)
    for j in range(N):
        X = mx_ref.quantize(x[j])
        lg = mx_ref.matmul(X, mx_ref.quantize(rt[j]))[:, :N]
        m = lg.max(axis=1, keepdims=True)
        for e in range(N):
            y[j] = y[j] + (lg[:, e:e + 1] == m) * (mx_ref.matmul(X, W[e]) * m)
    return {"y": y}

@@ -1,0 +1,202 @@
+from concourse.bass import DstId, RemoteDMATransfer
+from concourse.mybir import dt, AluOpType, AxisListType, ActivationFunctionType
+
+N = 8
+NC = 128
+
+BLOCK_DIRECT = False
+
+SCRATCH = {
+    "wb": ("sbuf", [128, 4 * NC], "bfloat16"),
+    "xb": ("sbuf", [128, 4 * NC], "bfloat16"),
+    "rb": ("sbuf", [128, 4 * NC], "bfloat16"),
+    "xq": ("sbuf", [128, NC], "float8_e4m3fn_x4"),
+    "xs": ("sbuf", [128, NC], "uint8"),
+    "rq": ("sbuf", [128, NC], "float8_e4m3fn_x4"),
+    "rs": ("sbuf", [128, NC], "uint8"),
+    "wq": ("sbuf", [128, N * NC], "float8_e4m3fn_x4"),
+    "ws": ("sbuf", [128, N * NC], "uint8"),
+    "m": ("sbuf", [128, 1], "float32"),
+    "sel": ("sbuf", [128, N], "float32"),
+    "tl": ("sbuf", [128, 4 * NC], "float32"),
+    "tf": ("sbuf", [128, 4 * NC], "float32"),
+    "u": ("sbuf", [128, 2 * NC], "float32"),
+    "acc": ("sbuf", [128, NC], "float32"),
+    "pl": ("psum", [128, 512], "float32"),
+    "ph": ("psum", [128, 512], "float32"),
+    "pf0": ("psum", [128, 512], "float32"),
+    "pf1": ("psum", [128, 512], "float32"),
+    "pf2": ("psum", [128, 512], "float32"),
+    "pf3": ("psum", [128, 512], "float32"),
+}
+SEMAPHORES = (["ldw", "ldx", "ldr", "wrdy", "xrdy", "rrdy", "lg", "srdy", "hrdy", "ah", "vc", "sent", "stored"]
+              + ["c%d" % s for s in range(N)] + ["s%d" % s for s in range(N)]
+              + ["p%d" % k for k in range(4)] + ["a%d" % k for k in range(4)])
+
+
+def _count(mask):
+    return bin(mask).count("1")
+
+
+def _plan(cores, topo):
+    role, order = {}, []
+    for ch in sorted(set(topo.chip(c) for c in cores)):
+        home = [c for c in cores if topo.chip(c) == ch]
+        away = [c for c in cores if topo.chip(c) != ch]
+        gates = [c for c in home if all(topo.may_write(c, d) for d in away)]
+        plain = [c for c in home if c not in gates]
+        for c in home:
+            role[c] = {"home": home, "away": away, "gates": gates, "plain": plain}
+        order += plain + gates
+    slot = dict((c, i) for i, c in enumerate(order))
+
+    def engines(src, dests):
+        m = topo.mask(src, dests[0])
+        for d in dests[1:]:
+            m &= topo.mask(src, d)
+        return m
+
+    def twin(c, group):
+        return [d for d in group if topo.die(d) == topo.die(c)][0]
+
+    steps, far = {}, {}
+    for c in cores:
+        r, s = role[c], slot[c]
+        o = role[r["away"][0]]
+        peers = sorted([d for d in r["home"] if d != c], key=lambda d: topo.die(d) != topo.die(c))
+        blk_home = (slot[r["plain"][0]], slot[r["plain"][0]] + len(r["plain"]))
+        blk_away = (slot[o["plain"][0]], slot[o["plain"][0]] + len(o["plain"]))
+        st = []
+        if c in r["plain"]:
+            gs = [d for d in peers if d in r["gates"]]
+            rest = [d for d in peers if d not in gs]
+            st.append((["wrdy"], "c", s, s + 1, [(gs, engines(c, gs))]))
+            st.append(([], "s", s, s + 1, [(gs + rest, engines(c, gs + rest))]))
+            st.append(([], "c", s, s + 1, [(rest, engines(c, rest))]))
+            if not BLOCK_DIRECT:
+                to = [twin(c, r["gates"])]
+                for k in "cs":
+                    st.append((["%s%d" % (k, blk_away[0])], k, blk_away[0], blk_away[1], [(to, engines(c, to))]))
+        else:
+            fg = [twin(c, o["gates"])]
+            out = engines(c, fg)
+            for k in "cs":
+                st.append((["wrdy"] if k == "c" else [], k, s, s + 1,
+                           [(fg, out), (peers, engines(c, peers) & ~out)]))
+            to = [twin(c, o["plain"])] + (fg if BLOCK_DIRECT else [])
+            for k in "cs":
+                st.append((["%s%d" % (k, slot[p]) for p in r["plain"]], k, blk_home[0], blk_home[1],
+                           [(to, engines(c, to))]))
+            t = slot[fg[0]]
+            for k in "cs":
+                st.append((["%s%d" % (k, t)], k, t, t + 1, [(peers, engines(c, peers))]))
+        steps[c] = st
+        og = sorted(o["gates"], key=lambda d: topo.die(d) != topo.die(c))
+        far[c] = [(slot[d], slot[d]) for d in og] + [(b, blk_away[0]) for b in range(*blk_away)]
+    due = {}
+    for c in cores:
+        for _, k, lo, _, parts in steps[c]:
+            for dests, mask in parts:
+                for d in dests:
+                    key = (d, "%s%d" % (k, lo))
+                    due[key] = due.get(key, 0) + _count(mask)
+    return order, steps, due, far
+
+
+def rank_program(g, core, T, topo):
+    if T.rank_of(core) is None:
+        return
+    order, steps, due, far = _plan(T.cores, topo)
+    sem = T.sem
+    me = order.index(core)
+    home = [s for s in range(N) if topo.chip(order[s]) == topo.chip(core)]
+    h0, h1 = home[0], home[-1] + 1
+
+    def cols(lo, hi):
+        return slice(lo * NC, hi * NC)
+
+    def col_of(s):
+        e = T.rank_of(order[s])
+        return T.sel[:, e:e + 1]
+
+    g.sync.dma_start(T.wb[:], T.w[:]).then_inc(sem.ldw, 16)
+    g.sync.dma_start(T.xb[:], T.x[:]).then_inc(sem.ldx, 16)
+    g.sync.dma_start(T.rb[:], T.rt[:]).then_inc(sem.ldr, 16)
+
+    v = g.vector
+    v.wait_ge(sem.ldw, 16)
+    v.quantize_mx(T.wq[:, cols(me, me + 1)], T.ws[:, cols(me, me + 1)], T.wb[:]).then_inc(sem.wrdy, 1)
+    v.wait_ge(sem.ldx, 16)
+    v.quantize_mx(T.xq[:], T.xs[:], T.xb[:]).then_inc(sem.xrdy, 1)
+    v.wait_ge(sem.ldr, 16)
+    v.quantize_mx(T.rq[:], T.rs[:], T.rb[:]).then_inc(sem.rrdy, 1)
+
+    sent = 0
+    for waits, kind, lo, hi, parts in steps[core]:
+        for w in waits:
+            g.wait_ge(sem[w], 1 if w == "wrdy" else due[(core, w)])
+
+        def view():
+            return T.wq[:, cols(lo, hi)].bitcast(dt.uint8) if kind == "c" else T.ws[:, cols(lo, hi)]
+        trs = []
+        for dests, mask in parts:
+            ids = [DstId(rid=topo.addr(d)[0], pnc=topo.addr(d)[1]) for d in dests]
+            trs.append(RemoteDMATransfer(dst_ids=ids, dma_engine_mask=mask, remote_sem=sem["%s%d" % (kind, lo)],
+                                         srcs=[view()], dsts=[view() for _ in dests]))
+            sent += _count(mask)
+        g.remote_dma_fused(trs, local_sem=sem.sent)
+    g.wait_ge(sem.sent, sent)
+
+    te = g.tensor
+
+    def arrived(s):
+        for k in "cs":
+            te.wait_ge(sem["%s%d" % (k, s)], due[(core, "%s%d" % (k, s))])
+    te.wait_ge(sem.xrdy, 1)
+    te.wait_ge(sem.rrdy, 1)
+    te.matmul_mx(T.pl[:, 0:NC], T.xq[:], T.xs[:], T.rq[:], T.rs[:], True, True).then_inc(sem.lg, 1)
+    te.wait_ge(sem.wrdy, 1)
+    for s in home:
+        if s != me:
+            arrived(s)
+    te.matmul_mx(T.ph[:, 0:(h1 - h0) * NC], T.xq[:], T.xs[:], T.wq[:, cols(h0, h1)], T.ws[:, cols(h0, h1)],
+                 True, True).then_inc(sem.hrdy, 1)
+    for k, (s, tag) in enumerate(far[core]):
+        arrived(tag)
+        te.matmul_mx(T["pf%d" % k][:, 0:NC], T.xq[:], T.xs[:], T.wq[:, cols(s, s + 1)], T.ws[:, cols(s, s + 1)],
+                     True, True).then_inc(sem["p%d" % k], 1)
+
+    nv = 0
+    v.wait_ge(sem.lg, 1)
+    v.tensor_reduce(T.m[:, 0:1], T.pl[:, 0:N], AxisListType.X, AluOpType.max).then_inc(sem.vc, 1)
+    nv += 1
+    v.wait_ge(sem.vc, nv)
+    v.tensor_scalar(T.sel[:], T.pl[:, 0:N], T.m[:, 0:1], T.m[:, 0:1], AluOpType.is_equal,
+                    AluOpType.mult).then_inc(sem.srdy, 1)
+
+    sc = g.scalar
+    sc.wait_ge(sem.srdy, 1)
+    sc.wait_ge(sem.hrdy, 1)
+    for i, s in enumerate(home):
+        sc.activation(T.tl[:, cols(i, i + 1)], T.ph[:, cols(i, i + 1)], ActivationFunctionType.Identity,
+                      scale=col_of(s)).then_inc(sem.ah, 1)
+    for k, (s, _) in enumerate(far[core]):
+        sc.wait_ge(sem["p%d" % k], 1)
+        sc.activation(T.tf[:, cols(k, k + 1)], T["pf%d" % k][:, 0:NC], ActivationFunctionType.Identity,
+                      scale=col_of(s)).then_inc(sem["a%d" % k], 1)
+
+    v.wait_ge(sem.ah, len(home))
+    v.tensor_tensor(T.u[:], T.tl[:, cols(0, 2)], T.tl[:, cols(2, 4)], AluOpType.add).then_inc(sem.vc, 1)
+    nv += 1
+    v.wait_ge(sem.vc, nv)
+    v.tensor_tensor(T.acc[:], T.u[:, cols(0, 1)], T.u[:, cols(1, 2)], AluOpType.add).then_inc(sem.vc, 1)
+    nv += 1
+    for k in range(len(far[core])):
+        v.wait_ge(sem["a%d" % k], 1)
+        v.wait_ge(sem.vc, nv)
+        v.tensor_tensor(T.acc[:], T.acc[:], T.tf[:, cols(k, k + 1)], AluOpType.add).then_inc(sem.vc, 1)
+        nv += 1
+
+    g.sync.wait_ge(sem.vc, nv)
+    g.sync.dma_start(T.y[:], T.acc[:]).then_inc(sem.stored, 16)
+    g.sync.wait_ge(sem.stored, 16)

@@ -4,7 +4,8 @@ from concourse.mybir import dt, AluOpType, AxisListType, ActivationFunctionType
 N = 8
 NC = 128
 
-BLOCK_DIRECT = False
+LAND1 = "pp"
+LAND2 = "pg"
 
 SCRATCH = {
     "wb": ("sbuf", [128, 4 * NC], "bfloat16"),
@@ -18,20 +19,20 @@ SCRATCH = {
     "ws": ("sbuf", [128, N * NC], "uint8"),
     "m": ("sbuf", [128, 1], "float32"),
     "sel": ("sbuf", [128, N], "float32"),
-    "tl": ("sbuf", [128, 4 * NC], "float32"),
-    "tf": ("sbuf", [128, 4 * NC], "float32"),
-    "u": ("sbuf", [128, 2 * NC], "float32"),
+    "t": ("sbuf", [128, N * NC], "float32"),
     "acc": ("sbuf", [128, NC], "float32"),
     "pl": ("psum", [128, 512], "float32"),
-    "ph": ("psum", [128, 512], "float32"),
-    "pf0": ("psum", [128, 512], "float32"),
-    "pf1": ("psum", [128, 512], "float32"),
-    "pf2": ("psum", [128, 512], "float32"),
-    "pf3": ("psum", [128, 512], "float32"),
+    "pg0": ("psum", [128, 512], "float32"),
+    "pg1": ("psum", [128, 512], "float32"),
+    "pg2": ("psum", [128, 512], "float32"),
+    "pg3": ("psum", [128, 512], "float32"),
+    "pg4": ("psum", [128, 512], "float32"),
+    "pg5": ("psum", [128, 512], "float32"),
+    "pg6": ("psum", [128, 512], "float32"),
 }
-SEMAPHORES = (["ldw", "ldx", "ldr", "wrdy", "xrdy", "rrdy", "lg", "srdy", "hrdy", "ah", "vc", "sent", "stored"]
+SEMAPHORES = (["ldw", "ldx", "ldr", "wrdy", "xrdy", "rrdy", "lg", "srdy", "vc", "sent", "stored"]
               + ["c%d" % s for s in range(N)] + ["s%d" % s for s in range(N)]
-              + ["p%d" % k for k in range(4)] + ["a%d" % k for k in range(4)])
+              + ["p%d" % k for k in range(7)] + ["a%d" % k for k in range(7)])
 
 
 def _count(mask):
@@ -59,58 +60,61 @@ def _plan(cores, topo):
     def twin(c, group):
         return [d for d in group if topo.die(d) == topo.die(c)][0]
 
-    steps, far = {}, {}
+    def peers_of(c):
+        return sorted([d for d in role[c]["home"] if d != c], key=lambda d: topo.die(d) != topo.die(c))
+
+    steps = dict((c, []) for c in cores)
+    groups = {}
+
+    def add(c, phase, waits, k, s, parts):
+        steps[c].append((phase, waits, k, s, parts))
+
     for c in cores:
         r, s = role[c], slot[c]
         o = role[r["away"][0]]
-        peers = sorted([d for d in r["home"] if d != c], key=lambda d: topo.die(d) != topo.die(c))
-        blk_home = (slot[r["plain"][0]], slot[r["plain"][0]] + len(r["plain"]))
-        blk_away = (slot[o["plain"][0]], slot[o["plain"][0]] + len(o["plain"]))
-        st = []
+        peers = peers_of(c)
         if c in r["plain"]:
-            gs = [d for d in peers if d in r["gates"]]
-            rest = [d for d in peers if d not in gs]
-            st.append((["wrdy"], "c", s, s + 1, [(gs, engines(c, gs))]))
-            st.append(([], "s", s, s + 1, [(gs + rest, engines(c, gs + rest))]))
-            st.append(([], "c", s, s + 1, [(rest, engines(c, rest))]))
-            if not BLOCK_DIRECT:
-                to = [twin(c, r["gates"])]
-                for k in "cs":
-                    st.append((["%s%d" % (k, blk_away[0])], k, blk_away[0], blk_away[1], [(to, engines(c, to))]))
+            first = [twin(c, r["gates"])]
+            later = [d for d in peers if d not in first]
+            add(c, 0, ["wrdy"], "c", s, [(first, engines(c, first))])
+            add(c, 0, [], "s", s, [(first + later, engines(c, peers))])
+            add(c, 0, [], "c", s, [(later, engines(c, later))])
         else:
-            fg = [twin(c, o["gates"])]
-            out = engines(c, fg)
-            for k in "cs":
-                st.append((["wrdy"] if k == "c" else [], k, s, s + 1,
-                           [(fg, out), (peers, engines(c, peers) & ~out)]))
-            to = [twin(c, o["plain"])] + (fg if BLOCK_DIRECT else [])
-            for k in "cs":
-                st.append((["%s%d" % (k, slot[p]) for p in r["plain"]], k, blk_home[0], blk_home[1],
-                           [(to, engines(c, to))]))
-            t = slot[fg[0]]
-            for k in "cs":
-                st.append((["%s%d" % (k, t)], k, t, t + 1, [(peers, engines(c, peers))]))
-        steps[c] = st
-        og = sorted(o["gates"], key=lambda d: topo.die(d) != topo.die(c))
-        far[c] = [(slot[d], slot[d]) for d in og] + [(b, blk_away[0]) for b in range(*blk_away)]
+            there = {"g": twin(c, o["gates"]), "p": twin(c, o["plain"])}
+            out = engines(c, [there["g"]])
+            a = slot[twin(c, r["plain"])]
+            for i, k in enumerate("cs"):
+                land = there[LAND1[i]]
+                add(c, 0, ["wrdy"] if k == "c" else [], k, s, [([land], out), (peers, engines(c, peers) & ~out)])
+                add(land, 2, ["%s%d" % (k, s)], k, s, [(peers_of(land), engines(land, peers_of(land)))])
+                land = there[LAND2[i]]
+                add(c, 1, ["%s%d" % (k, a)], k, a, [([land], out)])
+                add(land, 3, ["%s%d" % (k, a)], k, a, [(peers_of(land), engines(land, peers_of(land)))])
+        near = lambda d: topo.die(d) != topo.die(c)
+        hp = [slot[d] for d in r["plain"]]
+        gr = [(s, s + 1)] if c in r["gates"] else []
+        gr += [(hp[0], hp[-1] + 1)]
+        gr += [(slot[d], slot[d] + 1) for d in sorted(r["gates"], key=near) if d != c]
+        gr += [(slot[d], slot[d] + 1) for d in sorted(o["gates"], key=near)]
+        gr += [(slot[d], slot[d] + 1) for d in sorted(o["plain"], key=near)]
+        groups[c] = gr
     due = {}
     for c in cores:
-        for _, k, lo, _, parts in steps[c]:
+        steps[c] = sorted(steps[c], key=lambda st: st[0])
+        for _, _, k, s, parts in steps[c]:
             for dests, mask in parts:
                 for d in dests:
-                    key = (d, "%s%d" % (k, lo))
+                    key = (d, "%s%d" % (k, s))
                     due[key] = due.get(key, 0) + _count(mask)
-    return order, steps, due, far
+    return order, steps, due, groups
 
 
 def rank_program(g, core, T, topo):
     if T.rank_of(core) is None:
         return
-    order, steps, due, far = _plan(T.cores, topo)
+    order, steps, due, groups = _plan(T.cores, topo)
     sem = T.sem
     me = order.index(core)
-    home = [s for s in range(N) if topo.chip(order[s]) == topo.chip(core)]
-    h0, h1 = home[0], home[-1] + 1
 
     def cols(lo, hi):
         return slice(lo * NC, hi * NC)
@@ -132,39 +136,34 @@ def rank_program(g, core, T, topo):
     v.quantize_mx(T.rq[:], T.rs[:], T.rb[:]).then_inc(sem.rrdy, 1)
 
     sent = 0
-    for waits, kind, lo, hi, parts in steps[core]:
+    for _, waits, kind, s, parts in steps[core]:
         for w in waits:
             g.wait_ge(sem[w], 1 if w == "wrdy" else due[(core, w)])
 
         def view():
-            return T.wq[:, cols(lo, hi)].bitcast(dt.uint8) if kind == "c" else T.ws[:, cols(lo, hi)]
+            return T.wq[:, cols(s, s + 1)].bitcast(dt.uint8) if kind == "c" else T.ws[:, cols(s, s + 1)]
         trs = []
         for dests, mask in parts:
             ids = [DstId(rid=topo.addr(d)[0], pnc=topo.addr(d)[1]) for d in dests]
-            trs.append(RemoteDMATransfer(dst_ids=ids, dma_engine_mask=mask, remote_sem=sem["%s%d" % (kind, lo)],
+            trs.append(RemoteDMATransfer(dst_ids=ids, dma_engine_mask=mask, remote_sem=sem["%s%d" % (kind, s)],
                                          srcs=[view()], dsts=[view() for _ in dests]))
             sent += _count(mask)
         g.remote_dma_fused(trs, local_sem=sem.sent)
     g.wait_ge(sem.sent, sent)
 
     te = g.tensor
-
-    def arrived(s):
-        for k in "cs":
-            te.wait_ge(sem["%s%d" % (k, s)], due[(core, "%s%d" % (k, s))])
     te.wait_ge(sem.xrdy, 1)
     te.wait_ge(sem.rrdy, 1)
     te.matmul_mx(T.pl[:, 0:NC], T.xq[:], T.xs[:], T.rq[:], T.rs[:], True, True).then_inc(sem.lg, 1)
-    te.wait_ge(sem.wrdy, 1)
-    for s in home:
-        if s != me:
-            arrived(s)
-    te.matmul_mx(T.ph[:, 0:(h1 - h0) * NC], T.xq[:], T.xs[:], T.wq[:, cols(h0, h1)], T.ws[:, cols(h0, h1)],
-                 True, True).then_inc(sem.hrdy, 1)
-    for k, (s, tag) in enumerate(far[core]):
-        arrived(tag)
-        te.matmul_mx(T["pf%d" % k][:, 0:NC], T.xq[:], T.xs[:], T.wq[:, cols(s, s + 1)], T.ws[:, cols(s, s + 1)],
-                     True, True).then_inc(sem["p%d" % k], 1)
+    for i, (lo, hi) in enumerate(groups[core]):
+        for s in range(lo, hi):
+            if s == me:
+                te.wait_ge(sem.wrdy, 1)
+            else:
+                for k in "cs":
+                    te.wait_ge(sem["%s%d" % (k, s)], due[(core, "%s%d" % (k, s))])
+        te.matmul_mx(T["pg%d" % i][:, 0:(hi - lo) * NC], T.xq[:], T.xs[:], T.wq[:, cols(lo, hi)], T.ws[:, cols(lo, hi)],
+                     True, True).then_inc(sem["p%d" % i], 1)
 
     nv = 0
     v.wait_ge(sem.lg, 1)
@@ -176,26 +175,25 @@ def rank_program(g, core, T, topo):
 
     sc = g.scalar
     sc.wait_ge(sem.srdy, 1)
-    sc.wait_ge(sem.hrdy, 1)
-    for i, s in enumerate(home):
-        sc.activation(T.tl[:, cols(i, i + 1)], T.ph[:, cols(i, i + 1)], ActivationFunctionType.Identity,
-                      scale=col_of(s)).then_inc(sem.ah, 1)
-    for k, (s, _) in enumerate(far[core]):
-        sc.wait_ge(sem["p%d" % k], 1)
-        sc.activation(T.tf[:, cols(k, k + 1)], T["pf%d" % k][:, 0:NC], ActivationFunctionType.Identity,
-                      scale=col_of(s)).then_inc(sem["a%d" % k], 1)
+    for i, (lo, hi) in enumerate(groups[core]):
+        sc.wait_ge(sem["p%d" % i], 1)
+        for s in range(lo, hi):
+            sc.activation(T.t[:, cols(s, s + 1)], T["pg%d" % i][:, cols(s - lo, s - lo + 1)],
+                          ActivationFunctionType.Identity, scale=col_of(s)).then_inc(sem["a%d" % i], 1)
 
-    v.wait_ge(sem.ah, len(home))
-    v.tensor_tensor(T.u[:], T.tl[:, cols(0, 2)], T.tl[:, cols(2, 4)], AluOpType.add).then_inc(sem.vc, 1)
-    nv += 1
-    v.wait_ge(sem.vc, nv)
-    v.tensor_tensor(T.acc[:], T.u[:, cols(0, 1)], T.u[:, cols(1, 2)], AluOpType.add).then_inc(sem.vc, 1)
-    nv += 1
-    for k in range(len(far[core])):
-        v.wait_ge(sem["a%d" % k], 1)
-        v.wait_ge(sem.vc, nv)
-        v.tensor_tensor(T.acc[:], T.acc[:], T.tf[:, cols(k, k + 1)], AluOpType.add).then_inc(sem.vc, 1)
-        nv += 1
+    prev = None
+    started = False
+    for i, (lo, hi) in enumerate(groups[core]):
+        v.wait_ge(sem["a%d" % i], hi - lo)
+        for s in range(lo, hi):
+            if prev is None:
+                prev = s
+                continue
+            v.wait_ge(sem.vc, nv)
+            first = T.acc[:] if started else T.t[:, cols(prev, prev + 1)]
+            v.tensor_tensor(T.acc[:], first, T.t[:, cols(s, s + 1)], AluOpType.add).then_inc(sem.vc, 1)
+            started = True
+            nv += 1
 
     g.sync.wait_ge(sem.vc, nv)
     g.sync.dma_start(T.y[:], T.acc[:]).then_inc(sem.stored, 16)

from concourse.bass import DstId, RemoteDMATransfer
from concourse.mybir import dt, AluOpType, AxisListType, ActivationFunctionType

N = 8
NC = 128

LAND1 = "pp"
LAND2 = "pg"

SCRATCH = {
    "wb": ("sbuf", [128, 4 * NC], "bfloat16"),
    "xb": ("sbuf", [128, 4 * NC], "bfloat16"),
    "rb": ("sbuf", [128, 4 * NC], "bfloat16"),
    "xq": ("sbuf", [128, NC], "float8_e4m3fn_x4"),
    "xs": ("sbuf", [128, NC], "uint8"),
    "rq": ("sbuf", [128, NC], "float8_e4m3fn_x4"),
    "rs": ("sbuf", [128, NC], "uint8"),
    "wq": ("sbuf", [128, N * NC], "float8_e4m3fn_x4"),
    "ws": ("sbuf", [128, N * NC], "uint8"),
    "m": ("sbuf", [128, 1], "float32"),
    "sel": ("sbuf", [128, N], "float32"),
    "t": ("sbuf", [128, N * NC], "float32"),
    "acc": ("sbuf", [128, NC], "float32"),
    "pl": ("psum", [128, 512], "float32"),
    "pg0": ("psum", [128, 512], "float32"),
    "pg1": ("psum", [128, 512], "float32"),
    "pg2": ("psum", [128, 512], "float32"),
    "pg3": ("psum", [128, 512], "float32"),
    "pg4": ("psum", [128, 512], "float32"),
    "pg5": ("psum", [128, 512], "float32"),
    "pg6": ("psum", [128, 512], "float32"),
}
SEMAPHORES = (["ldw", "ldx", "ldr", "wrdy", "xrdy", "rrdy", "lg", "srdy", "vc", "sent", "stored"]
              + ["c%d" % s for s in range(N)] + ["s%d" % s for s in range(N)]
              + ["p%d" % k for k in range(7)] + ["a%d" % k for k in range(7)])


def _count(mask):
    return bin(mask).count("1")


def _plan(cores, topo):
    role, order = {}, []
    for ch in sorted(set(topo.chip(c) for c in cores)):
        home = [c for c in cores if topo.chip(c) == ch]
        away = [c for c in cores if topo.chip(c) != ch]
        gates = [c for c in home if all(topo.may_write(c, d) for d in away)]
        plain = [c for c in home if c not in gates]
        for c in home:
            role[c] = {"home": home, "away": away, "gates": gates, "plain": plain}
        order += plain + gates
    slot = dict((c, i) for i, c in enumerate(order))

    def engines(src, dests):
        m = topo.mask(src, dests[0])
        for d in dests[1:]:
            m &= topo.mask(src, d)
        return m

    def twin(c, group):
        return [d for d in group if topo.die(d) == topo.die(c)][0]

    def peers_of(c):
        return sorted([d for d in role[c]["home"] if d != c], key=lambda d: topo.die(d) != topo.die(c))

    steps = dict((c, []) for c in cores)
    groups = {}

    def add(c, phase, waits, k, s, parts):
        steps[c].append((phase, waits, k, s, parts))

    for c in cores:
        r, s = role[c], slot[c]
        o = role[r["away"][0]]
        peers = peers_of(c)
        if c in r["plain"]:
            first = [twin(c, r["gates"])]
            later = [d for d in peers if d not in first]
            add(c, 0, ["wrdy"], "c", s, [(first, engines(c, first))])
            add(c, 0, [], "s", s, [(first + later, engines(c, peers))])
            add(c, 0, [], "c", s, [(later, engines(c, later))])
        else:
            there = {"g": twin(c, o["gates"]), "p": twin(c, o["plain"])}
            out = engines(c, [there["g"]])
            a = slot[twin(c, r["plain"])]
            for i, k in enumerate("cs"):
                land = there[LAND1[i]]
                add(c, 0, ["wrdy"] if k == "c" else [], k, s, [([land], out), (peers, engines(c, peers) & ~out)])
                add(land, 2, ["%s%d" % (k, s)], k, s, [(peers_of(land), engines(land, peers_of(land)))])
                land = there[LAND2[i]]
                add(c, 1, ["%s%d" % (k, a)], k, a, [([land], out)])
                add(land, 3, ["%s%d" % (k, a)], k, a, [(peers_of(land), engines(land, peers_of(land)))])
        near = lambda d: topo.die(d) != topo.die(c)
        hp = [slot[d] for d in r["plain"]]
        gr = [(s, s + 1)] if c in r["gates"] else []
        gr += [(hp[0], hp[-1] + 1)]
        gr += [(slot[d], slot[d] + 1) for d in sorted(r["gates"], key=near) if d != c]
        gr += [(slot[d], slot[d] + 1) for d in sorted(o["gates"], key=near)]
        gr += [(slot[d], slot[d] + 1) for d in sorted(o["plain"], key=near)]
        groups[c] = gr
    due = {}
    for c in cores:
        steps[c] = sorted(steps[c], key=lambda st: st[0])
        for _, _, k, s, parts in steps[c]:
            for dests, mask in parts:
                for d in dests:
                    key = (d, "%s%d" % (k, s))
                    due[key] = due.get(key, 0) + _count(mask)
    return order, steps, due, groups


def rank_program(g, core, T, topo):
    if T.rank_of(core) is None:
        return
    order, steps, due, groups = _plan(T.cores, topo)
    sem = T.sem
    me = order.index(core)

    def cols(lo, hi):
        return slice(lo * NC, hi * NC)

    def col_of(s):
        e = T.rank_of(order[s])
        return T.sel[:, e:e + 1]

    g.sync.dma_start(T.wb[:], T.w[:]).then_inc(sem.ldw, 16)
    g.sync.dma_start(T.xb[:], T.x[:]).then_inc(sem.ldx, 16)
    g.sync.dma_start(T.rb[:], T.rt[:]).then_inc(sem.ldr, 16)

    v = g.vector
    v.wait_ge(sem.ldw, 16)
    v.quantize_mx(T.wq[:, cols(me, me + 1)], T.ws[:, cols(me, me + 1)], T.wb[:]).then_inc(sem.wrdy, 1)
    v.wait_ge(sem.ldx, 16)
    v.quantize_mx(T.xq[:], T.xs[:], T.xb[:]).then_inc(sem.xrdy, 1)
    v.wait_ge(sem.ldr, 16)
    v.quantize_mx(T.rq[:], T.rs[:], T.rb[:]).then_inc(sem.rrdy, 1)

    sent = 0
    for _, waits, kind, s, parts in steps[core]:
        for w in waits:
            g.wait_ge(sem[w], 1 if w == "wrdy" else due[(core, w)])

        def view():
            return T.wq[:, cols(s, s + 1)].bitcast(dt.uint8) if kind == "c" else T.ws[:, cols(s, s + 1)]
        trs = []
        for dests, mask in parts:
            ids = [DstId(rid=topo.addr(d)[0], pnc=topo.addr(d)[1]) for d in dests]
            trs.append(RemoteDMATransfer(dst_ids=ids, dma_engine_mask=mask, remote_sem=sem["%s%d" % (kind, s)],
                                         srcs=[view()], dsts=[view() for _ in dests]))
            sent += _count(mask)
        g.remote_dma_fused(trs, local_sem=sem.sent)
    g.wait_ge(sem.sent, sent)

    te = g.tensor
    te.wait_ge(sem.xrdy, 1)
    te.wait_ge(sem.rrdy, 1)
    te.matmul_mx(T.pl[:, 0:NC], T.xq[:], T.xs[:], T.rq[:], T.rs[:], True, True).then_inc(sem.lg, 1)
    for i, (lo, hi) in enumerate(groups[core]):
        for s in range(lo, hi):
            if s == me:
                te.wait_ge(sem.wrdy, 1)
            else:
                for k in "cs":
                    te.wait_ge(sem["%s%d" % (k, s)], due[(core, "%s%d" % (k, s))])
        te.matmul_mx(T["pg%d" % i][:, 0:(hi - lo) * NC], T.xq[:], T.xs[:], T.wq[:, cols(lo, hi)], T.ws[:, cols(lo, hi)],
                     True, True).then_inc(sem["p%d" % i], 1)

    nv = 0
    v.wait_ge(sem.lg, 1)
    v.tensor_reduce(T.m[:, 0:1], T.pl[:, 0:N], AxisListType.X, AluOpType.max).then_inc(sem.vc, 1)
    nv += 1
    v.wait_ge(sem.vc, nv)
    v.tensor_scalar(T.sel[:], T.pl[:, 0:N], T.m[:, 0:1], T.m[:, 0:1], AluOpType.is_equal,
                    AluOpType.mult).then_inc(sem.srdy, 1)

    sc = g.scalar
    sc.wait_ge(sem.srdy, 1)
    for i, (lo, hi) in enumerate(groups[core]):
        sc.wait_ge(sem["p%d" % i], 1)
        for s in range(lo, hi):
            sc.activation(T.t[:, cols(s, s + 1)], T["pg%d" % i][:, cols(s - lo, s - lo + 1)],
                          ActivationFunctionType.Identity, scale=col_of(s)).then_inc(sem["a%d" % i], 1)

    prev = None
    started = False
    for i, (lo, hi) in enumerate(groups[core]):
        v.wait_ge(sem["a%d" % i], hi - lo)
        for s in range(lo, hi):
            if prev is None:
                prev = s
                continue
            v.wait_ge(sem.vc, nv)
            first = T.acc[:] if started else T.t[:, cols(prev, prev + 1)]
            v.tensor_tensor(T.acc[:], first, T.t[:, cols(s, s + 1)], AluOpType.add).then_inc(sem.vc, 1)
            started = True
            nv += 1

    g.sync.wait_ge(sem.vc, nv)
    g.sync.dma_start(T.y[:], T.acc[:]).then_inc(sem.stored, 16)
    g.sync.wait_ge(sem.stored, 16)
